import numpy as np
import ml_dtypes


def mxq(x, axis, fmt="e4m3"):
    dtype, down = {"e4m3": (ml_dtypes.float8_e4m3fn, 7), "e5m2": (ml_dtypes.float8_e5m2, 14)}[fmt]
    v = np.moveaxis(np.asarray(x, np.float32).astype(ml_dtypes.bfloat16).astype(np.float64), axis, -1)
    blocks = v.reshape(v.shape[:-1] + (-1, 32))
    amax = np.abs(blocks).max(-1, keepdims=True)
    byte = np.maximum(np.where(amax > 0, np.frexp(amax)[1] - 1 + 127, 0) - down, 1)
    scale = np.exp2(byte - 127.0)
    codes = (blocks / scale).astype(np.float32).astype(dtype).astype(np.float64)
    return np.moveaxis((codes * scale).reshape(v.shape), -1, axis)


WIDE = False


def mx_kscale(k):
    if not WIDE:
        return np.ones(k)
    levels = np.array([10, -10, 5, -5, 0])
    if k % 512:
        return np.exp2(np.random.permutation(np.resize(levels, k // 32))).repeat(32)
    a = np.empty((k // 512, 16))
    for p in range(k // 512):
        a[p, :8] = np.random.permutation(np.resize(levels, 8))
        for g in range(8):
            far = levels[np.abs(levels - a[p, g]) >= 10]
            a[p, g + 8] = far[np.random.randint(len(far))]
    return np.exp2(a.ravel()).repeat(32)


def f64(x):
    return np.asarray(x).astype(np.float64)


def striped(idx):
    return np.tile(idx.reshape(-1, 16).T, (8, 1)).astype(np.uint16)


def unstriped(offs):
    return offs[:16].T.reshape(-1).astype(np.int64)


def striped8(idx):
    return np.concatenate([x.reshape(-1, 16).T for x in idx]).astype(np.uint16)


def runs(offs, k):
    lists = np.stack([offs[16 * r : 16 * r + 16].T.reshape(-1) for r in range(8)]).astype(np.int64)
    return lists[np.arange(k) % 512 // 64]


def pack_weight(w):
    k, n = w.shape
    w = f64(np.asarray(w, np.float32).astype(ml_dtypes.bfloat16)).reshape(k // 32, 32, n)
    amax = np.abs(w).max(1)
    byte = np.clip(np.where(amax > 0, np.frexp(amax)[1] - 1 + 127 - 7, 1), 1, 254)
    scaled = (w * np.exp2(127.0 - byte)[:, None, :]).reshape(k, n).astype(np.float32)
    words = np.ascontiguousarray(scaled.reshape(k // 512, 128, 4, n).transpose(0, 1, 3, 2)).astype(ml_dtypes.float8_e4m3fn).view(np.uint8)
    return words, np.ascontiguousarray(byte.astype(np.uint8).reshape(k // 512, 16, n))


def unpack_weight(words, scales):
    g, p, n, _ = words.shape
    vals = np.ascontiguousarray(words).view(ml_dtypes.float8_e4m3fn).astype(np.float64) * np.repeat(np.exp2(scales.astype(np.float64) - 127.0), 8, axis=1)[..., None]
    return vals.transpose(0, 1, 3, 2).reshape(g * 512, n)

def planes(y):
    n, m = y.shape
    v = y.astype(np.float32).astype(ml_dtypes.bfloat16).astype(np.float64).reshape(n // 32, 32, m)
    top = np.abs(v).max(1)
    byte = np.clip(np.where(top > 0, np.frexp(top)[1] - 1 + 127 - 7, 1), 1, 254)
    codes = (v * np.exp2(127.0 - byte)[:, None, :]).reshape(n, m).astype(np.float32).astype(ml_dtypes.float8_e4m3fn).view(np.uint8)
    words = codes.reshape(n // 512, 128, 4, m).transpose(0, 1, 3, 2)
    return np.ascontiguousarray(words), np.ascontiguousarray(byte.astype(np.uint8).reshape(n // 512, 16, m))


K, T, S, H, J, G = 512, 2048, 512, 512, 512, 2048


def setup_inputs():
    n = np.random.standard_normal
    s = mx_kscale(K)[:, None]
    packed_xT = pack_weight(n((K, T)) * s)
    packed_w1 = pack_weight(n((K, H)) / np.sqrt(K) / s)
    packed_dT = pack_weight(n((K, G)) / s)
    return {
        "x_words": packed_xT[0],
        "x_scales": packed_xT[1],
        "w1_words": packed_w1[0],
        "w1_scales": packed_w1[1],
        "tab": n((H, J)).astype(np.float32),
        "gs": (np.random.uniform(0.5, 1.5, (K, 1)) * s).astype(np.float32),
        "d_words": packed_dT[0],
        "d_scales": packed_dT[1],
        "offs": striped(np.random.permutation(T)[:S]),
        "n1": striped8(np.random.randint(0, J, (8, S))),
        "n2": striped8(np.stack([np.random.permutation(S) for _ in range(8)])),
        "k1": striped8(np.random.randint(0, G, (8, H))),
        "n3": striped(np.random.permutation(S)),
        "n4": striped(np.random.permutation(S)),
    }


def reference(x_words, x_scales, w1_words, w1_scales, tab, gs, d_words, d_scales, offs, n1, n2, k1, n3, n4):
    d_k1 = unpack_weight(d_words, d_scales)[np.arange(K)[:, None], runs(k1, K)]
    xq = unpack_weight(x_words, x_scales)[:, unstriped(offs)]
    y = unpack_weight(w1_words, w1_scales).T @ xq
    z = f64(gs) * (np.abs(y - (y[np.arange(H)[:, None], runs(n2, H)]) - (f64(tab)[np.arange(H)[:, None], runs(n1, H)])))
    h = 0.0625 * ((d_k1.T @ mxq(z, 0, "e4m3")))
    out_0 = (np.tanh(h[:, unstriped(n3)] - h)) * h[:, unstriped(n4)]
    return (out_0,) + planes(out_0)

@@ -1,0 +1,212 @@
+from contextlib import ExitStack
+
+import concourse.mybir as mybir
+
+F32 = mybir.dt.float32
+BF16 = mybir.dt.bfloat16
+I32 = mybir.dt.int32
+U32 = mybir.dt.uint32
+U16 = mybir.dt.uint16
+U8 = mybir.dt.uint8
+FP8X4 = mybir.dt.float8_e4m3fn_x4
+ACT = mybir.ActivationFunctionType
+ALU = mybir.AluOpType
+
+P = 128
+PACK = 4
+S = 512
+T = 2048
+FLOPS = 2 * 2 * 512 * 512 * 512
+
+CHUNKS_Z = ((0, 256), (256, 128), (384, 128))
+CHUNKS_OUT = ((0, 256), (256, 128), (384, 128))
+SIGN_COLS = 128
+
+
+def entries(list_tile, first, count):
+    return list_tile[:, first // 16 : (first + count) // 16]
+
+
+def tile_picked_densekinddfdif_none_po_kernel(
+    tc, x_words, x_scales, w1_words, w1_scales, tab, gs, d_words, d_scales, offs, n1, n2, k1, n3, n4, out_0, out_1, out_2
+):
+    nc = tc.nc
+    with ExitStack() as ctx:
+        keep = ctx.enter_context(tc.tile_pool(name="keep", bufs=1))
+        psum = ctx.enter_context(tc.psum_pool(name="psum", bufs=1))
+
+        def sb(name, shape, dtype):
+            return keep.tile(shape, dtype, name=name, align_bytes=64)
+
+        def bank(number, width, name):
+            return psum.tile([P, width], F32, name=name, tag="bank%d" % number)
+
+        lists = {}
+        for name in ("offs", "n1", "n2", "k1", "n3", "n4"):
+            lists[name] = sb("list_" + name, [P, S // 16], U16)
+
+        x_win = sb("x_win", [P, T], U32)
+        xs_win = sb("xs_win", [P, T], U8)
+        d_win = sb("d_win", [P, T], U32)
+        ds_win = sb("ds_win", [P, T], U8)
+        w_raw = sb("w_raw", [P, S], U32)
+        ws_raw = sb("ws_raw", [P, S], U8)
+        ds_placed = sb("ds_placed", [P, S], U8)
+        tabs = [sb("tab%d" % t, [P, S], F32) for t in range(PACK)]
+        gs_sb = sb("gs_sb", [P, PACK], F32)
+
+        for plane in (xs_win, ws_raw, ds_win, ds_placed):
+            nc.vector.memset(plane[:].bitcast(I32), 0)
+
+        def words(dram):
+            return dram[0].rearrange("p n r -> p (n r)").bitcast(I32)
+
+        tab_rows = tab.rearrange("(p t) c -> p t c", t=PACK)
+
+        nc.sync.dma_start(lists["offs"][:], offs)
+        for q in range(4):
+            nc.sync.dma_start(xs_win[32 * q : 32 * q + 4, :].bitcast(I32), x_scales[0, 4 * q : 4 * q + 4, :].bitcast(I32))
+        nc.sync.dma_start(lists["n1"][:], n1)
+        nc.sync.dma_start(tabs[0][:], tab_rows[:, 0, :])
+        nc.sync.dma_start(tabs[1][:], tab_rows[:, 1, :])
+        nc.sync.dma_start(x_win[:].bitcast(I32), words(x_words))
+        nc.sync.dma_start(w_raw[:].bitcast(I32), words(w1_words))
+        nc.sync.dma_start(lists["k1"][:], k1)
+        nc.sync.dma_start(tabs[2][:], tab_rows[:, 2, :])
+        nc.sync.dma_start(tabs[3][:], tab_rows[:, 3, :])
+        nc.sync.dma_start(lists["n2"][:], n2)
+        nc.sync.dma_start(d_win[:].bitcast(I32), words(d_words))
+        nc.sync.dma_start(lists["n3"][:], n3)
+        nc.sync.dma_start(lists["n4"][:], n4)
+
+        for q in range(4):
+            nc.gpsimd.dma_start(ws_raw[32 * q : 32 * q + 4, :].bitcast(I32), w1_scales[0, 4 * q : 4 * q + 4, :].bitcast(I32))
+        nc.gpsimd.dma_start(gs_sb[:], gs.rearrange("(p t) o -> p (t o)", t=PACK))
+        for e in range(2):
+            nc.gpsimd.dma_start(ds_win[e:P:16, :].bitcast(I32), d_scales[0, e:16:2, :].bitcast(I32))
+
+        def deal(name, src, dtype, view):
+            dealt = sb(name, [P, S], dtype)
+            dst_ap = dealt[:] if view == dtype else dealt[:].bitcast(view)
+            src_ap = src[:] if view == dtype else src[:].bitcast(view)
+            nc.vector.tensor_copy(
+                dst_ap.rearrange("p (t m) -> p m t", t=PACK), src_ap.rearrange("p (m t) -> p m t", t=PACK)
+            )
+            return dealt
+
+        xs_picked = sb("xs_picked", [P, S], U8)
+        nc.vector.tensor_copy(xs_picked[:], xs_win[:].indirect(lists["offs"][:]))
+        x_picked = sb("x_picked", [P, S], U32)
+        nc.vector.tensor_copy(x_picked[:], x_win[:].indirect(lists["offs"][:]))
+        ws_dealt = deal("ws_dealt", ws_raw, U8, U8)
+        w_dealt = deal("w_dealt", w_raw, U32, I32)
+
+        kind = sb("kind", [P, PACK, S], F32)
+
+        def fetch_kind(t):
+            for c0 in (0, S // 2):
+                src = tabs[t][:].indirect(entries(lists["n1"], c0, S // 2))
+                if t < 2:
+                    nc.scalar.activation(kind[:, t, c0 : c0 + S // 2], src, ACT.Copy)
+                else:
+                    nc.vector.tensor_copy(kind[:, t, c0 : c0 + S // 2], src)
+
+        fetch_kind(0)
+        fetch_kind(1)
+        sign = sb("sign", [P, SIGN_COLS, PACK], BF16)
+        nc.scalar.activation(sign[:], gs_sb[:].unsqueeze(1).to_broadcast([P, SIGN_COLS, PACK]), ACT.Sign)
+
+        ys = []
+        for t in range(PACK):
+            acc = bank(t, S, "y_acc%d" % t)
+            cols = slice(t * P, (t + 1) * P)
+            nc.tensor.matmul_mx(
+                out=acc[:], lhsT=w_dealt[:, cols].bitcast(FP8X4), lhsT_scale=ws_dealt[:, cols],
+                rhs=x_picked[:].bitcast(FP8X4), rhs_scale=xs_picked[:], start=True, stop=True,
+            )
+            y = sb("y%d" % t, [P, S], F32)
+            nc.scalar.activation(y[:], acc[:], ACT.Copy, scale=gs_sb[:, t : t + 1])
+            ys.append(y)
+
+        fetch_kind(2)
+        fetch_kind(3)
+        part = sb("part", [P, PACK, S], F32)
+        for t in range(PACK):
+            nc.vector.scalar_tensor_tensor(
+                part[:, t, :], kind[:, t, :], gs_sb[:, t : t + 1], ys[t][:], ALU.mult, ALU.subtract
+            )
+
+        ds_picked = sb("ds_picked", [P, S], U8)
+        nc.vector.tensor_copy(ds_picked[:], ds_win[:].indirect(lists["k1"][:]))
+        ds_dealt = deal("ds_dealt", ds_picked, U8, U8)
+        for r, src_row in enumerate((0, 1, 16, 17)):
+            nc.gpsimd.dma_start(ds_placed[r:P:32, :].bitcast(I32), ds_dealt[src_row:P:32, :].bitcast(I32))
+        d_picked = sb("d_picked", [P, S], U32)
+        nc.vector.tensor_copy(d_picked[:], d_win[:].indirect(lists["k1"][:]))
+        d_dealt = deal("d_dealt", d_picked, U32, I32)
+
+        def four_at_a_time_out(tile):
+            return tile[:].rearrange("p (c i) t -> p c t i", i=4)
+
+        def four_at_a_time_in(tile):
+            return tile[:].rearrange("p t (c i) -> p c t i", i=4)
+
+        h = sb("h", [P, PACK, S], F32)
+        for ci, (c0, cw) in enumerate(CHUNKS_Z):
+            other = sb("other%d" % ci, [P, PACK, cw], F32)
+            diff = sb("diff%d" % ci, [P, PACK, cw], F32)
+            for t in range(PACK):
+                nc.scalar.activation(other[:, t, :], ys[t][:].indirect(entries(lists["n2"], c0, cw)), ACT.Copy)
+                nc.vector.tensor_tensor(diff[:, t, :], part[:, t, c0 : c0 + cw], other[:, t, :], ALU.add)
+            size = sb("size%d" % ci, [P, cw, PACK], BF16)
+            nc.scalar.activation(four_at_a_time_out(size), four_at_a_time_in(diff), ACT.Abs)
+            z = sb("z%d" % ci, [P, cw * PACK], BF16)
+            reps = cw // SIGN_COLS
+            nc.vector.tensor_tensor(
+                z[:].rearrange("p (r e) -> p r e", r=reps),
+                size[:].rearrange("p (r c) t -> p r (c t)", r=reps),
+                sign[:].rearrange("p c t -> p (c t)").unsqueeze(1).to_broadcast([P, reps, SIGN_COLS * PACK]),
+                ALU.mult,
+            )
+            z_words = sb("z_words%d" % ci, [P, cw], U32)
+            z_scales = sb("z_scales%d" % ci, [P, cw], U8)
+            nc.vector.quantize_mx(out=z_words[:].bitcast(FP8X4), scales=z_scales[:], in_=z[:])
+            for t in range(PACK):
+                acc = bank((4 * (ci + 1) + t) % 8, cw, "h_acc%d_%d" % (ci, t))
+                cols = slice(t * P, (t + 1) * P)
+                nc.tensor.matmul_mx(
+                    out=acc[:], lhsT=d_dealt[:, cols].bitcast(FP8X4), lhsT_scale=ds_placed[:, cols],
+                    rhs=z_words[:].bitcast(FP8X4), rhs_scale=z_scales[:], start=True, stop=True,
+                )
+                if ci == len(CHUNKS_Z) - 1 and t % 2 == 1:
+                    nc.vector.tensor_scalar_mul(h[:, t, c0 : c0 + cw], acc[:], 0.0625)
+                else:
+                    nc.scalar.activation(h[:, t, c0 : c0 + cw], acc[:], ACT.Copy, scale=0.0625)
+
+        out_rows = out_0.rearrange("(p t) c -> p t c", t=PACK)
+        out_words = out_1[0].rearrange("p n r -> p (n r)").bitcast(I32)
+        o_scales = sb("o_scales", [P, S], U8)
+        for ci, (c0, cw) in enumerate(CHUNKS_OUT):
+            near = sb("near%d" % ci, [P, PACK, cw], F32)
+            gap = sb("gap%d" % ci, [P, PACK, cw], F32)
+            far = sb("far%d" % ci, [P, PACK, cw], F32)
+            bent = sb("bent%d" % ci, [P, PACK, cw], F32)
+            res = sb("res%d" % ci, [P, PACK, cw], F32)
+            for t in range(PACK):
+                nc.vector.tensor_copy(near[:, t, :], h[:, t, :].indirect(entries(lists["n3"], c0, cw)))
+                nc.scalar.activation(far[:, t, :], h[:, t, :].indirect(entries(lists["n4"], c0, cw)), ACT.Copy)
+                if t % 2 == 1:
+                    pair = slice(t - 1, t + 1)
+                    nc.vector.tensor_tensor(gap[:, pair, :], near[:, pair, :], h[:, pair, c0 : c0 + cw], ALU.subtract)
+                    nc.scalar.activation(bent[:, pair, :], gap[:, pair, :], ACT.Tanh)
+                    nc.vector.tensor_tensor(res[:, pair, :], bent[:, pair, :], far[:, pair, :], ALU.mult)
+            nc.sync.dma_start(out_rows[:, :, c0 : c0 + cw], res[:])
+            rounded = sb("rounded%d" % ci, [P, cw, PACK], BF16)
+            nc.vector.tensor_copy(four_at_a_time_out(rounded), four_at_a_time_in(res))
+            o_words = sb("o_words%d" % ci, [P, cw], U32)
+            nc.vector.quantize_mx(
+                out=o_words[:].bitcast(FP8X4), scales=o_scales[:, c0 : c0 + cw], in_=rounded[:].rearrange("p c t -> p (c t)")
+            )
+            nc.sync.dma_start(out_words[:, c0 : c0 + cw], o_words[:].bitcast(I32))
+        for q in range(4):
+            nc.sync.dma_start(out_2[0, 4 * q : 4 * q + 4, :].bitcast(I32), o_scales[32 * q : 32 * q + 4, :].bitcast(I32))

@@ -17,10 +17,9 @@ PACK = 4
 S = 512
 T = 2048
 FLOPS = 2 * 2 * 512 * 512 * 512
-
-CHUNKS_Z = ((0, 256), (256, 128), (384, 128))
-CHUNKS_OUT = ((0, 256), (256, 128), (384, 128))
-SIGN_COLS = 128
+CW = 128
+NCH = S // CW
+HALF = S // 2
 
 
 def entries(list_tile, first, count):
@@ -35,8 +34,8 @@ def tile_picked_densekinddfdif_none_po_kernel(
         keep = ctx.enter_context(tc.tile_pool(name="keep", bufs=1))
         psum = ctx.enter_context(tc.psum_pool(name="psum", bufs=1))
 
-        def sb(name, shape, dtype):
-            return keep.tile(shape, dtype, name=name, align_bytes=64)
+        def sb(name, shape, dtype, tag=None):
+            return keep.tile(shape, dtype, name=name, tag=tag or name, align_bytes=64)
 
         def bank(number, width, name):
             return psum.tile([P, width], F32, name=name, tag="bank%d" % number)
@@ -55,95 +54,44 @@ def tile_picked_densekinddfdif_none_po_kernel(
         tabs = [sb("tab%d" % t, [P, S], F32) for t in range(PACK)]
         gs_sb = sb("gs_sb", [P, PACK], F32)
 
-        for plane in (xs_win, ws_raw, ds_win, ds_placed):
+        nc.gpsimd.memset(xs_win[:].bitcast(I32), 0)
+        for plane in (ds_win, ws_raw, ds_placed):
             nc.vector.memset(plane[:].bitcast(I32), 0)
+
+        warm = sb("warm", [P, 8], F32)
+        warm_out = sb("warm_out", [P, 8], F32)
+        nc.vector.memset(warm[:], 0.0)
+        nc.scalar.activation(warm_out[:], warm[:], ACT.Copy)
 
         def words(dram):
             return dram[0].rearrange("p n r -> p (n r)").bitcast(I32)
 
         tab_rows = tab.rearrange("(p t) c -> p t c", t=PACK)
 
+        nc.sync.dma_start(tabs[0][:], tab_rows[:, 0, :])
+        nc.sync.dma_start(lists["n1"][:], n1)
         nc.sync.dma_start(lists["offs"][:], offs)
         for q in range(4):
             nc.sync.dma_start(xs_win[32 * q : 32 * q + 4, :].bitcast(I32), x_scales[0, 4 * q : 4 * q + 4, :].bitcast(I32))
-        nc.sync.dma_start(lists["n1"][:], n1)
-        nc.sync.dma_start(tabs[0][:], tab_rows[:, 0, :])
-        nc.sync.dma_start(tabs[1][:], tab_rows[:, 1, :])
         nc.sync.dma_start(x_win[:].bitcast(I32), words(x_words))
         nc.sync.dma_start(w_raw[:].bitcast(I32), words(w1_words))
-        nc.sync.dma_start(lists["k1"][:], k1)
-        nc.sync.dma_start(tabs[2][:], tab_rows[:, 2, :])
-        nc.sync.dma_start(tabs[3][:], tab_rows[:, 3, :])
+        for q in range(4):
+            nc.sync.dma_start(ws_raw[32 * q : 32 * q + 4, :].bitcast(I32), w1_scales[0, 4 * q : 4 * q + 4, :].bitcast(I32))
+        for t in range(1, PACK):
+            nc.sync.dma_start(tabs[t][:], tab_rows[:, t, :])
         nc.sync.dma_start(lists["n2"][:], n2)
+        nc.sync.dma_start(lists["k1"][:], k1)
         nc.sync.dma_start(d_win[:].bitcast(I32), words(d_words))
         nc.sync.dma_start(lists["n3"][:], n3)
         nc.sync.dma_start(lists["n4"][:], n4)
 
-        for q in range(4):
-            nc.gpsimd.dma_start(ws_raw[32 * q : 32 * q + 4, :].bitcast(I32), w1_scales[0, 4 * q : 4 * q + 4, :].bitcast(I32))
+        nc.gpsimd.dma_start(ds_win[0:P:8, :].bitcast(I32), d_scales[0].bitcast(I32))
         nc.gpsimd.dma_start(gs_sb[:], gs.rearrange("(p t) o -> p (t o)", t=PACK))
-        for e in range(2):
-            nc.gpsimd.dma_start(ds_win[e:P:16, :].bitcast(I32), d_scales[0, e:16:2, :].bitcast(I32))
 
-        def deal(name, src, dtype, view):
-            dealt = sb(name, [P, S], dtype)
-            dst_ap = dealt[:] if view == dtype else dealt[:].bitcast(view)
-            src_ap = src[:] if view == dtype else src[:].bitcast(view)
+        def deal(dst_ap, src_ap):
             nc.vector.tensor_copy(
                 dst_ap.rearrange("p (t m) -> p m t", t=PACK), src_ap.rearrange("p (m t) -> p m t", t=PACK)
             )
-            return dealt
-
-        xs_picked = sb("xs_picked", [P, S], U8)
-        nc.vector.tensor_copy(xs_picked[:], xs_win[:].indirect(lists["offs"][:]))
-        x_picked = sb("x_picked", [P, S], U32)
-        nc.vector.tensor_copy(x_picked[:], x_win[:].indirect(lists["offs"][:]))
-        ws_dealt = deal("ws_dealt", ws_raw, U8, U8)
-        w_dealt = deal("w_dealt", w_raw, U32, I32)
-
-        kind = sb("kind", [P, PACK, S], F32)
-
-        def fetch_kind(t):
-            for c0 in (0, S // 2):
-                src = tabs[t][:].indirect(entries(lists["n1"], c0, S // 2))
-                if t < 2:
-                    nc.scalar.activation(kind[:, t, c0 : c0 + S // 2], src, ACT.Copy)
-                else:
-                    nc.vector.tensor_copy(kind[:, t, c0 : c0 + S // 2], src)
-
-        fetch_kind(0)
-        fetch_kind(1)
-        sign = sb("sign", [P, SIGN_COLS, PACK], BF16)
-        nc.scalar.activation(sign[:], gs_sb[:].unsqueeze(1).to_broadcast([P, SIGN_COLS, PACK]), ACT.Sign)
-
-        ys = []
-        for t in range(PACK):
-            acc = bank(t, S, "y_acc%d" % t)
-            cols = slice(t * P, (t + 1) * P)
-            nc.tensor.matmul_mx(
-                out=acc[:], lhsT=w_dealt[:, cols].bitcast(FP8X4), lhsT_scale=ws_dealt[:, cols],
-                rhs=x_picked[:].bitcast(FP8X4), rhs_scale=xs_picked[:], start=True, stop=True,
-            )
-            y = sb("y%d" % t, [P, S], F32)
-            nc.scalar.activation(y[:], acc[:], ACT.Copy, scale=gs_sb[:, t : t + 1])
-            ys.append(y)
-
-        fetch_kind(2)
-        fetch_kind(3)
-        part = sb("part", [P, PACK, S], F32)
-        for t in range(PACK):
-            nc.vector.scalar_tensor_tensor(
-                part[:, t, :], kind[:, t, :], gs_sb[:, t : t + 1], ys[t][:], ALU.mult, ALU.subtract
-            )
-
-        ds_picked = sb("ds_picked", [P, S], U8)
-        nc.vector.tensor_copy(ds_picked[:], ds_win[:].indirect(lists["k1"][:]))
-        ds_dealt = deal("ds_dealt", ds_picked, U8, U8)
-        for r, src_row in enumerate((0, 1, 16, 17)):
-            nc.gpsimd.dma_start(ds_placed[r:P:32, :].bitcast(I32), ds_dealt[src_row:P:32, :].bitcast(I32))
-        d_picked = sb("d_picked", [P, S], U32)
-        nc.vector.tensor_copy(d_picked[:], d_win[:].indirect(lists["k1"][:]))
-        d_dealt = deal("d_dealt", d_picked, U32, I32)
 
         def four_at_a_time_out(tile):
             return tile[:].rearrange("p (c i) t -> p c t i", i=4)
@@ -151,62 +99,137 @@ def tile_picked_densekinddfdif_none_po_kernel(
         def four_at_a_time_in(tile):
             return tile[:].rearrange("p t (c i) -> p c t i", i=4)
 
-        h = sb("h", [P, PACK, S], F32)
-        for ci, (c0, cw) in enumerate(CHUNKS_Z):
-            other = sb("other%d" % ci, [P, PACK, cw], F32)
-            diff = sb("diff%d" % ci, [P, PACK, cw], F32)
-            for t in range(PACK):
-                nc.scalar.activation(other[:, t, :], ys[t][:].indirect(entries(lists["n2"], c0, cw)), ACT.Copy)
-                nc.vector.tensor_tensor(diff[:, t, :], part[:, t, c0 : c0 + cw], other[:, t, :], ALU.add)
-            size = sb("size%d" % ci, [P, cw, PACK], BF16)
-            nc.scalar.activation(four_at_a_time_out(size), four_at_a_time_in(diff), ACT.Abs)
-            z = sb("z%d" % ci, [P, cw * PACK], BF16)
-            reps = cw // SIGN_COLS
-            nc.vector.tensor_tensor(
-                z[:].rearrange("p (r e) -> p r e", r=reps),
-                size[:].rearrange("p (r c) t -> p r (c t)", r=reps),
-                sign[:].rearrange("p c t -> p (c t)").unsqueeze(1).to_broadcast([P, reps, SIGN_COLS * PACK]),
-                ALU.mult,
+        kind = [sb("kind%d" % half, [P, PACK, HALF], F32) for half in range(2)]
+        part = [sb("part%d" % half, [P, PACK, HALF], F32) for half in range(2)]
+
+        def fetch_kind(t, half):
+            src = tabs[t][:].indirect(entries(lists["n1"], half * HALF, HALF))
+            if t < 2:
+                nc.scalar.activation(kind[half][:, t, :], src, ACT.Copy)
+            else:
+                nc.vector.tensor_copy(kind[half][:, t, :], src)
+
+        def make_part(t, half):
+            nc.vector.scalar_tensor_tensor(
+                part[half][:, t, :], kind[half][:, t, :], gs_sb[:, t : t + 1],
+                ys[t][:, half * HALF : (half + 1) * HALF], ALU.mult, ALU.subtract,
             )
-            z_words = sb("z_words%d" % ci, [P, cw], U32)
-            z_scales = sb("z_scales%d" % ci, [P, cw], U8)
-            nc.vector.quantize_mx(out=z_words[:].bitcast(FP8X4), scales=z_scales[:], in_=z[:])
+
+        xs_picked = sb("xs_picked", [P, S], U8)
+        nc.vector.tensor_copy(xs_picked[:], xs_win[:].indirect(lists["offs"][:]))
+        x_picked = sb("x_picked", [P, S], U32)
+        nc.vector.tensor_copy(x_picked[:], x_win[:].indirect(lists["offs"][:]))
+
+        sign = sb("sign", [P, CW, PACK], BF16)
+        nc.scalar.activation(sign[:], gs_sb[:].unsqueeze(1).to_broadcast([P, CW, PACK]), ACT.Sign)
+
+        ys = []
+        ws_dealt = sb("ws_dealt", [P, S], U8, tag="x_win")
+        for t in range(PACK):
+            w_dealt = sb("w_dealt%d" % t, [P, P], U32)
+            cols = slice(t * P, (t + 1) * P)
+            nc.gpsimd.tensor_copy(w_dealt[:].bitcast(I32), w_raw[:].bitcast(I32).rearrange("p (m t) -> p t m", t=PACK)[:, t, :])
+            nc.vector.tensor_copy(ws_dealt[:, cols], ws_raw[:].rearrange("p (m t) -> p t m", t=PACK)[:, t, :])
+            acc = bank(t, S, "y_acc%d" % t)
+            nc.tensor.matmul_mx(
+                out=acc[:], lhsT=w_dealt[:].bitcast(FP8X4), lhsT_scale=ws_dealt[:, cols],
+                rhs=x_picked[:].bitcast(FP8X4), rhs_scale=xs_picked[:], start=True, stop=True,
+            )
+            y = sb("y%d" % t, [P, S], F32)
+            if False:
+                nc.vector.tensor_scalar_mul(y[:], acc[:], gs_sb[:, t : t + 1])
+            else:
+                nc.scalar.activation(y[:], acc[:], ACT.Copy, scale=gs_sb[:, t : t + 1])
+            ys.append(y)
+
+        ds_picked = sb("ds_picked", [P, S], U8, tag="ws_raw")
+        nc.vector.tensor_copy(ds_picked[:], ds_win[:].indirect(lists["k1"][:]))
+        ds_dealt = sb("ds_dealt", [P, S], U8)
+        deal(ds_dealt[:], ds_picked[:])
+        for r in range(4):
+            nc.sync.dma_start(ds_placed[r:P:32, :].bitcast(I32), ds_dealt[8 * r : P : 32, :].bitcast(I32))
+
+        for t in range(PACK):
+            fetch_kind(t, 0)
+        for t in range(PACK):
+            make_part(t, 0)
+
+        d_picked = sb("d_picked", [P, S], U32)
+        d_dealt = sb("d_dealt", [P, S], U32)
+
+        diff_tag = ("diff0", "d_picked", "diff2", "diff3")
+        h = sb("h", [P, PACK, S], F32)
+        for c in range(NCH):
+            c0 = c * CW
+            half, within = divmod(c0, HALF)
+            other = sb("other%d" % c, [P, PACK, CW], F32, tag=diff_tag[c - 2] if c >= 2 else None)
+            diff = sb("diff%d" % c, [P, PACK, CW], F32, tag=diff_tag[c])
             for t in range(PACK):
-                acc = bank((4 * (ci + 1) + t) % 8, cw, "h_acc%d_%d" % (ci, t))
-                cols = slice(t * P, (t + 1) * P)
-                nc.tensor.matmul_mx(
-                    out=acc[:], lhsT=d_dealt[:, cols].bitcast(FP8X4), lhsT_scale=ds_placed[:, cols],
-                    rhs=z_words[:].bitcast(FP8X4), rhs_scale=z_scales[:], start=True, stop=True,
-                )
-                if ci == len(CHUNKS_Z) - 1 and t % 2 == 1:
-                    nc.vector.tensor_scalar_mul(h[:, t, c0 : c0 + cw], acc[:], 0.0625)
+                nc.scalar.activation(other[:, t, :], ys[t][:].indirect(entries(lists["n2"], c0, CW)), ACT.Copy)
+                if t % 2 == 1:
+                    pair = slice(t - 1, t + 1)
+                    nc.vector.tensor_tensor(
+                        diff[:, pair, :], part[half][:, pair, within : within + CW], other[:, pair, :], ALU.add
+                    )
+            if c == 0:
+                nc.vector.tensor_copy(d_picked[:], d_win[:].indirect(lists["k1"][:]))
+                deal(d_dealt[:].bitcast(I32), d_picked[:].bitcast(I32))
+            size = sb("size%d" % c, [P, CW, PACK], BF16)
+            nc.scalar.activation(four_at_a_time_out(size), four_at_a_time_in(diff), ACT.Abs)
+            z = sb("z%d" % c, [P, CW, PACK], BF16)
+            nc.vector.tensor_tensor(z[:], size[:], sign[:], ALU.mult)
+            z_words = sb("z_words%d" % c, [P, CW], U32)
+            z_scales = sb("z_scales%d" % c, [P, CW], U8)
+            nc.vector.quantize_mx(
+                out=z_words[:].bitcast(FP8X4), scales=z_scales[:], in_=z[:].rearrange("p c t -> p (c t)")
+            )
+            for pair in range(2):
+                acc = bank((4 + 2 * c + pair) % 8, 2 * CW, "h_acc%d_%d" % (c, pair))
+                for u in range(2):
+                    cols = slice((2 * pair + u) * P, (2 * pair + u + 1) * P)
+                    nc.tensor.matmul_mx(
+                        out=acc[:, u * CW : (u + 1) * CW], lhsT=d_dealt[:, cols].bitcast(FP8X4), lhsT_scale=ds_placed[:, cols],
+                        rhs=z_words[:].bitcast(FP8X4), rhs_scale=z_scales[:], start=True, stop=True,
+                    )
+                dst = h[:, 2 * pair : 2 * pair + 2, c0 : c0 + CW]
+                src = acc[:].rearrange("p (u c) -> p u c", u=2)
+                if c >= 2 and pair == 1:
+                    nc.vector.tensor_scalar_mul(dst, src, 0.0625)
                 else:
-                    nc.scalar.activation(h[:, t, c0 : c0 + cw], acc[:], ACT.Copy, scale=0.0625)
+                    nc.scalar.activation(dst, src, ACT.Copy, scale=0.0625)
+            if c == 0:
+                for t in range(PACK):
+                    fetch_kind(t, 1)
+                for t in range(PACK):
+                    make_part(t, 1)
 
         out_rows = out_0.rearrange("(p t) c -> p t c", t=PACK)
         out_words = out_1[0].rearrange("p n r -> p (n r)").bitcast(I32)
         o_scales = sb("o_scales", [P, S], U8)
-        for ci, (c0, cw) in enumerate(CHUNKS_OUT):
-            near = sb("near%d" % ci, [P, PACK, cw], F32)
-            gap = sb("gap%d" % ci, [P, PACK, cw], F32)
-            far = sb("far%d" % ci, [P, PACK, cw], F32)
-            bent = sb("bent%d" % ci, [P, PACK, cw], F32)
-            res = sb("res%d" % ci, [P, PACK, cw], F32)
+        for c in range(NCH):
+            c0 = c * CW
+            near = sb("near%d" % c, [P, PACK, CW], F32, tag="bent%d" % (c - 2) if c >= 2 else None)
+            far = sb("far%d" % c, [P, PACK, CW], F32, tag="gap%d" % (c - 2) if c >= 2 else None)
+            gap = sb("gap%d" % c, [P, PACK, CW], F32)
+            bent = sb("bent%d" % c, [P, PACK, CW], F32)
+            res = sb("res%d" % c, [P, PACK, CW], F32)
             for t in range(PACK):
-                nc.vector.tensor_copy(near[:, t, :], h[:, t, :].indirect(entries(lists["n3"], c0, cw)))
-                nc.scalar.activation(far[:, t, :], h[:, t, :].indirect(entries(lists["n4"], c0, cw)), ACT.Copy)
-                if t % 2 == 1:
-                    pair = slice(t - 1, t + 1)
-                    nc.vector.tensor_tensor(gap[:, pair, :], near[:, pair, :], h[:, pair, c0 : c0 + cw], ALU.subtract)
-                    nc.scalar.activation(bent[:, pair, :], gap[:, pair, :], ACT.Tanh)
-                    nc.vector.tensor_tensor(res[:, pair, :], bent[:, pair, :], far[:, pair, :], ALU.mult)
-            nc.sync.dma_start(out_rows[:, :, c0 : c0 + cw], res[:])
-            rounded = sb("rounded%d" % ci, [P, cw, PACK], BF16)
-            nc.vector.tensor_copy(four_at_a_time_out(rounded), four_at_a_time_in(res))
-            o_words = sb("o_words%d" % ci, [P, cw], U32)
+                nc.vector.tensor_copy(near[:, t, :], h[:, t, :].indirect(entries(lists["n3"], c0, CW)))
+                nc.scalar.activation(far[:, t, :], h[:, t, :].indirect(entries(lists["n4"], c0, CW)), ACT.Copy)
+            nc.vector.tensor_tensor(gap[:], near[:], h[:, :, c0 : c0 + CW], ALU.subtract)
+            nc.scalar.activation(bent[:], gap[:], ACT.Tanh)
+            nc.vector.tensor_tensor(res[:], bent[:], far[:], ALU.mult)
+            nc.sync.dma_start(out_rows[:, :, c0 : c0 + CW], res[:])
+            rounded = sb("rounded%d" % c, [P, CW, PACK], BF16)
+            if c < NCH - 1:
+                nc.scalar.activation(four_at_a_time_out(rounded), four_at_a_time_in(res), ACT.Copy)
+            else:
+                nc.vector.tensor_copy(four_at_a_time_out(rounded), four_at_a_time_in(res))
+            o_words = sb("o_words%d" % c, [P, CW], U32)
             nc.vector.quantize_mx(
-                out=o_words[:].bitcast(FP8X4), scales=o_scales[:, c0 : c0 + cw], in_=rounded[:].rearrange("p c t -> p (c t)")
+                out=o_words[:].bitcast(FP8X4), scales=o_scales[:, c0 : c0 + CW], in_=rounded[:].rearrange("p c t -> p (c t)")
             )
-            nc.sync.dma_start(out_words[:, c0 : c0 + cw], o_words[:].bitcast(I32))
+            nc.sync.dma_start(out_words[:, c0 : c0 + CW], o_words[:].bitcast(I32))
         for q in range(4):
-            nc.sync.dma_start(out_2[0, 4 * q : 4 * q + 4, :].bitcast(I32), o_scales[32 * q : 32 * q + 4, :].bitcast(I32))
+            queue = nc.scalar if q % 2 == 0 else nc.sync
+            queue.dma_start(out_2[0, 4 * q : 4 * q + 4, :].bitcast(I32), o_scales[32 * q : 32 * q + 4, :].bitcast(I32))

@@ -75,9 +75,10 @@ def tile_picked_densekinddfdif_none_po_kernel(
             nc.sync.dma_start(xs_win[32 * q : 32 * q + 4, :].bitcast(I32), x_scales[0, 4 * q : 4 * q + 4, :].bitcast(I32))
         nc.sync.dma_start(x_win[:].bitcast(I32), words(x_words))
         nc.sync.dma_start(w_raw[:].bitcast(I32), words(w1_words))
+        nc.sync.dma_start(tabs[1][:], tab_rows[:, 1, :])
         for q in range(4):
             nc.sync.dma_start(ws_raw[32 * q : 32 * q + 4, :].bitcast(I32), w1_scales[0, 4 * q : 4 * q + 4, :].bitcast(I32))
-        for t in range(1, PACK):
+        for t in range(2, PACK):
             nc.sync.dma_start(tabs[t][:], tab_rows[:, t, :])
         nc.sync.dma_start(lists["n2"][:], n2)
         nc.sync.dma_start(lists["k1"][:], k1)
@@ -85,8 +86,8 @@ def tile_picked_densekinddfdif_none_po_kernel(
         nc.sync.dma_start(lists["n3"][:], n3)
         nc.sync.dma_start(lists["n4"][:], n4)
 
-        nc.gpsimd.dma_start(ds_win[0:P:8, :].bitcast(I32), d_scales[0].bitcast(I32))
         nc.gpsimd.dma_start(gs_sb[:], gs.rearrange("(p t) o -> p (t o)", t=PACK))
+        nc.gpsimd.dma_start(ds_win[0:P:8, :].bitcast(I32), d_scales[0].bitcast(I32))
 
         def deal(dst_ap, src_ap):
             nc.vector.tensor_copy(
@@ -96,15 +97,15 @@ def tile_picked_densekinddfdif_none_po_kernel(
         def four_at_a_time_out(tile):
             return tile[:].rearrange("p (c i) t -> p c t i", i=4)
 
-        def four_at_a_time_in(tile):
-            return tile[:].rearrange("p t (c i) -> p c t i", i=4)
+        def four_at_a_time_in(ap):
+            return ap.rearrange("p t (c i) -> p c t i", i=4)
 
         kind = [sb("kind%d" % half, [P, PACK, HALF], F32) for half in range(2)]
         part = [sb("part%d" % half, [P, PACK, HALF], F32) for half in range(2)]
 
         def fetch_kind(t, half):
             src = tabs[t][:].indirect(entries(lists["n1"], half * HALF, HALF))
-            if t < 2:
+            if t < 2 or (t == 2 and half == 1):
                 nc.scalar.activation(kind[half][:, t, :], src, ACT.Copy)
             else:
                 nc.vector.tensor_copy(kind[half][:, t, :], src)
@@ -120,8 +121,6 @@ def tile_picked_densekinddfdif_none_po_kernel(
         x_picked = sb("x_picked", [P, S], U32)
         nc.vector.tensor_copy(x_picked[:], x_win[:].indirect(lists["offs"][:]))
 
-        sign = sb("sign", [P, CW, PACK], BF16)
-        nc.scalar.activation(sign[:], gs_sb[:].unsqueeze(1).to_broadcast([P, CW, PACK]), ACT.Sign)
 
         ys = []
         ws_dealt = sb("ws_dealt", [P, S], U8, tag="x_win")
@@ -149,33 +148,33 @@ def tile_picked_densekinddfdif_none_po_kernel(
         for r in range(4):
             nc.sync.dma_start(ds_placed[r:P:32, :].bitcast(I32), ds_dealt[8 * r : P : 32, :].bitcast(I32))
 
-        for t in range(PACK):
-            fetch_kind(t, 0)
-        for t in range(PACK):
-            make_part(t, 0)
-
         d_picked = sb("d_picked", [P, S], U32)
         d_dealt = sb("d_dealt", [P, S], U32)
+        nc.vector.tensor_copy(d_picked[:], d_win[:].indirect(lists["k1"][:]))
+        deal(d_dealt[:].bitcast(I32), d_picked[:].bitcast(I32))
 
-        diff_tag = ("diff0", "d_picked", "diff2", "diff3")
-        h = sb("h", [P, PACK, S], F32)
-        for c in range(NCH):
-            c0 = c * CW
-            half, within = divmod(c0, HALF)
-            other = sb("other%d" % c, [P, PACK, CW], F32, tag=diff_tag[c - 2] if c >= 2 else None)
-            diff = sb("diff%d" % c, [P, PACK, CW], F32, tag=diff_tag[c])
+        for half in range(2):
             for t in range(PACK):
-                nc.scalar.activation(other[:, t, :], ys[t][:].indirect(entries(lists["n2"], c0, CW)), ACT.Copy)
-                if t % 2 == 1:
-                    pair = slice(t - 1, t + 1)
-                    nc.vector.tensor_tensor(
-                        diff[:, pair, :], part[half][:, pair, within : within + CW], other[:, pair, :], ALU.add
-                    )
-            if c == 0:
-                nc.vector.tensor_copy(d_picked[:], d_win[:].indirect(lists["k1"][:]))
-                deal(d_dealt[:].bitcast(I32), d_picked[:].bitcast(I32))
+                fetch_kind(t, half)
+        sign = sb("sign", [P, CW, PACK], BF16, tag="tab0")
+        nc.scalar.activation(sign[:], gs_sb[:].unsqueeze(1).to_broadcast([P, CW, PACK]), ACT.Sign)
+
+        diff = []
+        for half in range(2):
+            other = sb("other%d" % half, [P, PACK, HALF], F32)
+            diff.append(sb("diff%d" % half, [P, PACK, HALF], F32))
+            for t in range(PACK):
+                make_part(t, half)
+            for t in range(PACK):
+                nc.scalar.activation(other[:, t, :], ys[t][:].indirect(entries(lists["n2"], half * HALF, HALF)), ACT.Copy)
+            for t in range(PACK):
+                nc.vector.tensor_tensor(diff[half][:, t, :], part[half][:, t, :], other[:, t, :], ALU.add)
+
+        h_acc = []
+        for c in range(NCH):
+            half, within = divmod(c * CW, HALF)
             size = sb("size%d" % c, [P, CW, PACK], BF16)
-            nc.scalar.activation(four_at_a_time_out(size), four_at_a_time_in(diff), ACT.Abs)
+            nc.scalar.activation(four_at_a_time_out(size), four_at_a_time_in(diff[half][:, :, within : within + CW]), ACT.Abs)
             z = sb("z%d" % c, [P, CW, PACK], BF16)
             nc.vector.tensor_tensor(z[:], size[:], sign[:], ALU.mult)
             z_words = sb("z_words%d" % c, [P, CW], U32)
@@ -191,40 +190,42 @@ def tile_picked_densekinddfdif_none_po_kernel(
                         out=acc[:, u * CW : (u + 1) * CW], lhsT=d_dealt[:, cols].bitcast(FP8X4), lhsT_scale=ds_placed[:, cols],
                         rhs=z_words[:].bitcast(FP8X4), rhs_scale=z_scales[:], start=True, stop=True,
                     )
-                dst = h[:, 2 * pair : 2 * pair + 2, c0 : c0 + CW]
-                src = acc[:].rearrange("p (u c) -> p u c", u=2)
-                if c >= 2 and pair == 1:
+                h_acc.append(acc)
+
+        h = sb("h", [P, PACK, S], F32)
+        for c in range(NCH):
+            for pair in range(2):
+                dst = h[:, 2 * pair : 2 * pair + 2, c * CW : (c + 1) * CW]
+                src = h_acc[2 * c + pair][:].rearrange("p (u c) -> p u c", u=2)
+                if pair == 1:
                     nc.vector.tensor_scalar_mul(dst, src, 0.0625)
                 else:
                     nc.scalar.activation(dst, src, ACT.Copy, scale=0.0625)
-            if c == 0:
-                for t in range(PACK):
-                    fetch_kind(t, 1)
-                for t in range(PACK):
-                    make_part(t, 1)
 
         out_rows = out_0.rearrange("(p t) c -> p t c", t=PACK)
         out_words = out_1[0].rearrange("p n r -> p (n r)").bitcast(I32)
         o_scales = sb("o_scales", [P, S], U8)
         for c in range(NCH):
             c0 = c * CW
-            near = sb("near%d" % c, [P, PACK, CW], F32, tag="bent%d" % (c - 2) if c >= 2 else None)
-            far = sb("far%d" % c, [P, PACK, CW], F32, tag="gap%d" % (c - 2) if c >= 2 else None)
+            half, within = divmod(c0, HALF)
+            if within == 0:
+                near = sb("near%d" % half, [P, PACK, HALF], F32)
+                far = sb("far%d" % half, [P, PACK, HALF], F32)
+                for t in range(PACK):
+                    nc.vector.tensor_copy(near[:, t, :], h[:, t, :].indirect(entries(lists["n3"], c0, HALF)))
+                    nc.scalar.activation(far[:, t, :], h[:, t, :].indirect(entries(lists["n4"], c0, HALF)), ACT.Copy)
             gap = sb("gap%d" % c, [P, PACK, CW], F32)
             bent = sb("bent%d" % c, [P, PACK, CW], F32)
             res = sb("res%d" % c, [P, PACK, CW], F32)
-            for t in range(PACK):
-                nc.vector.tensor_copy(near[:, t, :], h[:, t, :].indirect(entries(lists["n3"], c0, CW)))
-                nc.scalar.activation(far[:, t, :], h[:, t, :].indirect(entries(lists["n4"], c0, CW)), ACT.Copy)
-            nc.vector.tensor_tensor(gap[:], near[:], h[:, :, c0 : c0 + CW], ALU.subtract)
+            nc.vector.tensor_tensor(gap[:], near[:, :, within : within + CW], h[:, :, c0 : c0 + CW], ALU.subtract)
             nc.scalar.activation(bent[:], gap[:], ACT.Tanh)
-            nc.vector.tensor_tensor(res[:], bent[:], far[:], ALU.mult)
+            nc.vector.tensor_tensor(res[:], bent[:], far[:, :, within : within + CW], ALU.mult)
             nc.sync.dma_start(out_rows[:, :, c0 : c0 + CW], res[:])
             rounded = sb("rounded%d" % c, [P, CW, PACK], BF16)
             if c < NCH - 1:
-                nc.scalar.activation(four_at_a_time_out(rounded), four_at_a_time_in(res), ACT.Copy)
+                nc.scalar.activation(four_at_a_time_out(rounded), four_at_a_time_in(res[:]), ACT.Copy)
             else:
-                nc.vector.tensor_copy(four_at_a_time_out(rounded), four_at_a_time_in(res))
+                nc.vector.tensor_copy(four_at_a_time_out(rounded), four_at_a_time_in(res[:]))
             o_words = sb("o_words%d" % c, [P, CW], U32)
             nc.vector.quantize_mx(
                 out=o_words[:].bitcast(FP8X4), scales=o_scales[:, c0 : c0 + CW], in_=rounded[:].rearrange("p c t -> p (c t)")

@@ -50,49 +50,42 @@ def tile_picked_densekinddfdif_none_po_kernel(
         ds_win = sb("ds_win", [P, T], U8)
         w_raw = sb("w_raw", [P, S], U32)
         ws_raw = sb("ws_raw", [P, S], U8)
-        ds_placed = sb("ds_placed", [P, S], U8)
         tabs = [sb("tab%d" % t, [P, S], F32) for t in range(PACK)]
         gs_sb = sb("gs_sb", [P, PACK], F32)
-
-        nc.gpsimd.memset(xs_win[:].bitcast(I32), 0)
-        for plane in (ds_win, ws_raw, ds_placed):
-            nc.vector.memset(plane[:].bitcast(I32), 0)
 
         warm = sb("warm", [P, 8], F32)
         warm_out = sb("warm_out", [P, 8], F32)
         nc.vector.memset(warm[:], 0.0)
         nc.scalar.activation(warm_out[:], warm[:], ACT.Copy)
 
+        nc.gpsimd.memset(xs_win[:].bitcast(I32), 0)
+        for plane in (ds_win, ws_raw):
+            nc.vector.memset(plane[:].bitcast(I32), 0)
+
         def words(dram):
             return dram[0].rearrange("p n r -> p (n r)").bitcast(I32)
 
         tab_rows = tab.rearrange("(p t) c -> p t c", t=PACK)
 
+        for name, dram in (("n1", n1), ("offs", offs), ("k1", k1)):
+            nc.sync.dma_start(lists[name][:], dram)
         nc.sync.dma_start(tabs[0][:], tab_rows[:, 0, :])
-        nc.sync.dma_start(lists["n1"][:], n1)
-        nc.sync.dma_start(lists["offs"][:], offs)
-        for q in range(4):
-            nc.sync.dma_start(xs_win[32 * q : 32 * q + 4, :].bitcast(I32), x_scales[0, 4 * q : 4 * q + 4, :].bitcast(I32))
+        for plane, dram in ((xs_win, x_scales), (ds_win, d_scales), (ws_raw, w1_scales)):
+            nc.sync.dma_start(plane[0:P:8, :].bitcast(I32), dram[0].bitcast(I32))
         nc.sync.dma_start(x_win[:].bitcast(I32), words(x_words))
         nc.sync.dma_start(w_raw[:].bitcast(I32), words(w1_words))
         nc.sync.dma_start(tabs[1][:], tab_rows[:, 1, :])
-        for q in range(4):
-            nc.sync.dma_start(ws_raw[32 * q : 32 * q + 4, :].bitcast(I32), w1_scales[0, 4 * q : 4 * q + 4, :].bitcast(I32))
+        nc.sync.dma_start(lists["n2"][:], n2)
         for t in range(2, PACK):
             nc.sync.dma_start(tabs[t][:], tab_rows[:, t, :])
-        nc.sync.dma_start(lists["n2"][:], n2)
-        nc.sync.dma_start(lists["k1"][:], k1)
         nc.sync.dma_start(d_win[:].bitcast(I32), words(d_words))
         nc.sync.dma_start(lists["n3"][:], n3)
         nc.sync.dma_start(lists["n4"][:], n4)
-
         nc.gpsimd.dma_start(gs_sb[:], gs.rearrange("(p t) o -> p (t o)", t=PACK))
-        nc.gpsimd.dma_start(ds_win[0:P:8, :].bitcast(I32), d_scales[0].bitcast(I32))
 
-        def deal(dst_ap, src_ap):
-            nc.vector.tensor_copy(
-                dst_ap.rearrange("p (t m) -> p m t", t=PACK), src_ap.rearrange("p (m t) -> p m t", t=PACK)
-            )
+        def place_rows(queue, plane):
+            for r in range(1, 4):
+                queue.dma_start(plane[r:P:32, :].bitcast(I32), plane[8 * r : P : 32, :].bitcast(I32))
 
         def four_at_a_time_out(tile):
             return tile[:].rearrange("p (c i) t -> p c t i", i=4)
@@ -118,46 +111,57 @@ def tile_picked_densekinddfdif_none_po_kernel(
 
         xs_picked = sb("xs_picked", [P, S], U8)
         nc.vector.tensor_copy(xs_picked[:], xs_win[:].indirect(lists["offs"][:]))
+        first_scales = sb("first_scales", [P, 2 * S], U8)
+        nc.vector.tensor_copy(first_scales[:, 0:S].bitcast(I32), xs_picked[:].bitcast(I32))
+        nc.gpsimd.tensor_copy(
+            first_scales[:, S : 2 * S].rearrange("p (t m) -> p t m", t=PACK), ws_raw[:].rearrange("p (m t) -> p t m", t=PACK)
+        )
+        place_rows(nc.scalar, first_scales)
         x_picked = sb("x_picked", [P, S], U32)
         nc.vector.tensor_copy(x_picked[:], x_win[:].indirect(lists["offs"][:]))
 
 
         ys = []
-        ws_dealt = sb("ws_dealt", [P, S], U8, tag="x_win")
         for t in range(PACK):
             w_dealt = sb("w_dealt%d" % t, [P, P], U32)
-            cols = slice(t * P, (t + 1) * P)
             nc.gpsimd.tensor_copy(w_dealt[:].bitcast(I32), w_raw[:].bitcast(I32).rearrange("p (m t) -> p t m", t=PACK)[:, t, :])
-            nc.vector.tensor_copy(ws_dealt[:, cols], ws_raw[:].rearrange("p (m t) -> p t m", t=PACK)[:, t, :])
             acc = bank(t, S, "y_acc%d" % t)
             nc.tensor.matmul_mx(
-                out=acc[:], lhsT=w_dealt[:].bitcast(FP8X4), lhsT_scale=ws_dealt[:, cols],
-                rhs=x_picked[:].bitcast(FP8X4), rhs_scale=xs_picked[:], start=True, stop=True,
+                out=acc[:], lhsT=w_dealt[:].bitcast(FP8X4), lhsT_scale=first_scales[:, S + t * P : S + (t + 1) * P],
+                rhs=x_picked[:].bitcast(FP8X4), rhs_scale=first_scales[:, 0:S], start=True, stop=True,
             )
             y = sb("y%d" % t, [P, S], F32)
-            if False:
+            if t == PACK - 1:
                 nc.vector.tensor_scalar_mul(y[:], acc[:], gs_sb[:, t : t + 1])
             else:
                 nc.scalar.activation(y[:], acc[:], ACT.Copy, scale=gs_sb[:, t : t + 1])
             ys.append(y)
 
-        ds_picked = sb("ds_picked", [P, S], U8, tag="ws_raw")
+        ds_picked = sb("ds_picked", [P, S], U8, tag="xs_picked")
         nc.vector.tensor_copy(ds_picked[:], ds_win[:].indirect(lists["k1"][:]))
-        ds_dealt = sb("ds_dealt", [P, S], U8)
-        deal(ds_dealt[:], ds_picked[:])
-        for r in range(4):
-            nc.sync.dma_start(ds_placed[r:P:32, :].bitcast(I32), ds_dealt[8 * r : P : 32, :].bitcast(I32))
+        ds_dealt = sb("ds_dealt", [P, S], U8, tag="x_win")
+        nc.vector.tensor_copy(
+            ds_dealt[:].rearrange("p (t m) -> p t m", t=PACK), ds_picked[:].rearrange("p (m t) -> p t m", t=PACK)
+        )
+        place_rows(nc.sync, ds_dealt)
 
         d_picked = sb("d_picked", [P, S], U32)
         d_dealt = sb("d_dealt", [P, S], U32)
         nc.vector.tensor_copy(d_picked[:], d_win[:].indirect(lists["k1"][:]))
-        deal(d_dealt[:].bitcast(I32), d_picked[:].bitcast(I32))
+        nc.vector.tensor_copy(
+            d_dealt[:].bitcast(I32).rearrange("p (t b i) -> p b t i", t=PACK, i=4),
+            d_picked[:].bitcast(I32).rearrange("p (b i t) -> p b t i", t=PACK, i=4),
+        )
 
         for half in range(2):
             for t in range(PACK):
                 fetch_kind(t, half)
-        sign = sb("sign", [P, CW, PACK], BF16, tag="tab0")
-        nc.scalar.activation(sign[:], gs_sb[:].unsqueeze(1).to_broadcast([P, CW, PACK]), ACT.Sign)
+        twice_not_negative = sb("twice_not_negative", [P, PACK], F32, tag="ws_raw")
+        nc.gpsimd.tensor_scalar(twice_not_negative[:], gs_sb[:], 0.0, 2.0, ALU.is_ge, ALU.mult)
+        sign = sb("sign", [P, CW, PACK], BF16, tag="w_raw")
+        nc.gpsimd.tensor_scalar(
+            sign[:], twice_not_negative[:].unsqueeze(1).to_broadcast([P, CW, PACK]), 1.0, -1.0, ALU.mult, ALU.add
+        )
 
         diff = []
         for half in range(2):
@@ -187,7 +191,7 @@ def tile_picked_densekinddfdif_none_po_kernel(
                 for u in range(2):
                     cols = slice((2 * pair + u) * P, (2 * pair + u + 1) * P)
                     nc.tensor.matmul_mx(
-                        out=acc[:, u * CW : (u + 1) * CW], lhsT=d_dealt[:, cols].bitcast(FP8X4), lhsT_scale=ds_placed[:, cols],
+                        out=acc[:, u * CW : (u + 1) * CW], lhsT=d_dealt[:, cols].bitcast(FP8X4), lhsT_scale=ds_dealt[:, cols],
                         rhs=z_words[:].bitcast(FP8X4), rhs_scale=z_scales[:], start=True, stop=True,
                     )
                 h_acc.append(acc)
@@ -197,13 +201,14 @@ def tile_picked_densekinddfdif_none_po_kernel(
             for pair in range(2):
                 dst = h[:, 2 * pair : 2 * pair + 2, c * CW : (c + 1) * CW]
                 src = h_acc[2 * c + pair][:].rearrange("p (u c) -> p u c", u=2)
-                if pair == 1:
+                if pair == 1 and c >= 2:
                     nc.vector.tensor_scalar_mul(dst, src, 0.0625)
                 else:
                     nc.scalar.activation(dst, src, ACT.Copy, scale=0.0625)
 
         out_rows = out_0.rearrange("(p t) c -> p t c", t=PACK)
         out_words = out_1[0].rearrange("p n r -> p (n r)").bitcast(I32)
+        o_words = sb("o_words", [P, S], U32)
         o_scales = sb("o_scales", [P, S], U8)
         for c in range(NCH):
             c0 = c * CW
@@ -212,7 +217,11 @@ def tile_picked_densekinddfdif_none_po_kernel(
                 near = sb("near%d" % half, [P, PACK, HALF], F32)
                 far = sb("far%d" % half, [P, PACK, HALF], F32)
                 for t in range(PACK):
-                    nc.vector.tensor_copy(near[:, t, :], h[:, t, :].indirect(entries(lists["n3"], c0, HALF)))
+                    picked = h[:, t, :].indirect(entries(lists["n3"], c0, HALF))
+                    if t == PACK - 1 and half == 0:
+                        nc.scalar.activation(near[:, t, :], picked, ACT.Copy)
+                    else:
+                        nc.vector.tensor_copy(near[:, t, :], picked)
                     nc.scalar.activation(far[:, t, :], h[:, t, :].indirect(entries(lists["n4"], c0, HALF)), ACT.Copy)
             gap = sb("gap%d" % c, [P, PACK, CW], F32)
             bent = sb("bent%d" % c, [P, PACK, CW], F32)
@@ -226,11 +235,12 @@ def tile_picked_densekinddfdif_none_po_kernel(
                 nc.scalar.activation(four_at_a_time_out(rounded), four_at_a_time_in(res[:]), ACT.Copy)
             else:
                 nc.vector.tensor_copy(four_at_a_time_out(rounded), four_at_a_time_in(res[:]))
-            o_words = sb("o_words%d" % c, [P, CW], U32)
             nc.vector.quantize_mx(
-                out=o_words[:].bitcast(FP8X4), scales=o_scales[:, c0 : c0 + CW], in_=rounded[:].rearrange("p c t -> p (c t)")
+                out=o_words[:, c0 : c0 + CW].bitcast(FP8X4), scales=o_scales[:, c0 : c0 + CW], in_=rounded[:].rearrange("p c t -> p (c t)")
             )
-            nc.sync.dma_start(out_words[:, c0 : c0 + CW], o_words[:].bitcast(I32))
+            if within > 0:
+                cols = slice(half * HALF, (half + 1) * HALF)
+                nc.sync.dma_start(out_words[:, cols], o_words[:, cols].bitcast(I32))
         for q in range(4):
             queue = nc.scalar if q % 2 == 0 else nc.sync
             queue.dma_start(out_2[0, 4 * q : 4 * q + 4, :].bitcast(I32), o_scales[32 * q : 32 * q + 4, :].bitcast(I32))

@@ -53,11 +53,6 @@ def tile_picked_densekinddfdif_none_po_kernel(
         tabs = [sb("tab%d" % t, [P, S], F32) for t in range(PACK)]
         gs_sb = sb("gs_sb", [P, PACK], F32)
 
-        warm = sb("warm", [P, 8], F32)
-        warm_out = sb("warm_out", [P, 8], F32)
-        nc.vector.memset(warm[:], 0.0)
-        nc.scalar.activation(warm_out[:], warm[:], ACT.Copy)
-
         nc.gpsimd.memset(xs_win[:].bitcast(I32), 0)
         for plane in (ds_win, ws_raw):
             nc.vector.memset(plane[:].bitcast(I32), 0)

from contextlib import ExitStack

import concourse.mybir as mybir

F32 = mybir.dt.float32
BF16 = mybir.dt.bfloat16
I32 = mybir.dt.int32
U32 = mybir.dt.uint32
U16 = mybir.dt.uint16
U8 = mybir.dt.uint8
FP8X4 = mybir.dt.float8_e4m3fn_x4
ACT = mybir.ActivationFunctionType
ALU = mybir.AluOpType

P = 128
PACK = 4
S = 512
T = 2048
FLOPS = 2 * 2 * 512 * 512 * 512
CW = 128
NCH = S // CW
HALF = S // 2


def entries(list_tile, first, count):
    return list_tile[:, first // 16 : (first + count) // 16]


def tile_picked_densekinddfdif_none_po_kernel(
    tc, x_words, x_scales, w1_words, w1_scales, tab, gs, d_words, d_scales, offs, n1, n2, k1, n3, n4, out_0, out_1, out_2
):
    nc = tc.nc
    with ExitStack() as ctx:
        keep = ctx.enter_context(tc.tile_pool(name="keep", bufs=1))
        psum = ctx.enter_context(tc.psum_pool(name="psum", bufs=1))

        def sb(name, shape, dtype, tag=None):
            return keep.tile(shape, dtype, name=name, tag=tag or name, align_bytes=64)

        def bank(number, width, name):
            return psum.tile([P, width], F32, name=name, tag="bank%d" % number)

        lists = {}
        for name in ("offs", "n1", "n2", "k1", "n3", "n4"):
            lists[name] = sb("list_" + name, [P, S // 16], U16)

        x_win = sb("x_win", [P, T], U32)
        xs_win = sb("xs_win", [P, T], U8)
        d_win = sb("d_win", [P, T], U32)
        ds_win = sb("ds_win", [P, T], U8)
        w_raw = sb("w_raw", [P, S], U32)
        ws_raw = sb("ws_raw", [P, S], U8)
        tabs = [sb("tab%d" % t, [P, S], F32) for t in range(PACK)]
        gs_sb = sb("gs_sb", [P, PACK], F32)

        nc.gpsimd.memset(xs_win[:].bitcast(I32), 0)
        for plane in (ds_win, ws_raw):
            nc.vector.memset(plane[:].bitcast(I32), 0)

        def words(dram):
            return dram[0].rearrange("p n r -> p (n r)").bitcast(I32)

        tab_rows = tab.rearrange("(p t) c -> p t c", t=PACK)

        for name, dram in (("n1", n1), ("offs", offs), ("k1", k1)):
            nc.sync.dma_start(lists[name][:], dram)
        nc.sync.dma_start(tabs[0][:], tab_rows[:, 0, :])
        for plane, dram in ((xs_win, x_scales), (ds_win, d_scales), (ws_raw, w1_scales)):
            nc.sync.dma_start(plane[0:P:8, :].bitcast(I32), dram[0].bitcast(I32))
        nc.sync.dma_start(x_win[:].bitcast(I32), words(x_words))
        nc.sync.dma_start(w_raw[:].bitcast(I32), words(w1_words))
        nc.sync.dma_start(tabs[1][:], tab_rows[:, 1, :])
        nc.sync.dma_start(lists["n2"][:], n2)
        for t in range(2, PACK):
            nc.sync.dma_start(tabs[t][:], tab_rows[:, t, :])
        nc.sync.dma_start(d_win[:].bitcast(I32), words(d_words))
        nc.sync.dma_start(lists["n3"][:], n3)
        nc.sync.dma_start(lists["n4"][:], n4)
        nc.gpsimd.dma_start(gs_sb[:], gs.rearrange("(p t) o -> p (t o)", t=PACK))

        def place_rows(queue, plane):
            for r in range(1, 4):
                queue.dma_start(plane[r:P:32, :].bitcast(I32), plane[8 * r : P : 32, :].bitcast(I32))

        def four_at_a_time_out(tile):
            return tile[:].rearrange("p (c i) t -> p c t i", i=4)

        def four_at_a_time_in(ap):
            return ap.rearrange("p t (c i) -> p c t i", i=4)

        kind = [sb("kind%d" % half, [P, PACK, HALF], F32) for half in range(2)]
        part = [sb("part%d" % half, [P, PACK, HALF], F32) for half in range(2)]

        def fetch_kind(t, half):
            src = tabs[t][:].indirect(entries(lists["n1"], half * HALF, HALF))
            if t < 2 or (t == 2 and half == 1):
                nc.scalar.activation(kind[half][:, t, :], src, ACT.Copy)
            else:
                nc.vector.tensor_copy(kind[half][:, t, :], src)

        def make_part(t, half):
            nc.vector.scalar_tensor_tensor(
                part[half][:, t, :], kind[half][:, t, :], gs_sb[:, t : t + 1],
                ys[t][:, half * HALF : (half + 1) * HALF], ALU.mult, ALU.subtract,
            )

        xs_picked = sb("xs_picked", [P, S], U8)
        nc.vector.tensor_copy(xs_picked[:], xs_win[:].indirect(lists["offs"][:]))
        first_scales = sb("first_scales", [P, 2 * S], U8)
        nc.vector.tensor_copy(first_scales[:, 0:S].bitcast(I32), xs_picked[:].bitcast(I32))
        nc.gpsimd.tensor_copy(
            first_scales[:, S : 2 * S].rearrange("p (t m) -> p t m", t=PACK), ws_raw[:].rearrange("p (m t) -> p t m", t=PACK)
        )
        place_rows(nc.scalar, first_scales)
        x_picked = sb("x_picked", [P, S], U32)
        nc.vector.tensor_copy(x_picked[:], x_win[:].indirect(lists["offs"][:]))


        ys = []
        for t in range(PACK):
            w_dealt = sb("w_dealt%d" % t, [P, P], U32)
            nc.gpsimd.tensor_copy(w_dealt[:].bitcast(I32), w_raw[:].bitcast(I32).rearrange("p (m t) -> p t m", t=PACK)[:, t, :])
            acc = bank(t, S, "y_acc%d" % t)
            nc.tensor.matmul_mx(
                out=acc[:], lhsT=w_dealt[:].bitcast(FP8X4), lhsT_scale=first_scales[:, S + t * P : S + (t + 1) * P],
                rhs=x_picked[:].bitcast(FP8X4), rhs_scale=first_scales[:, 0:S], start=True, stop=True,
            )
            y = sb("y%d" % t, [P, S], F32)
            if t == PACK - 1:
                nc.vector.tensor_scalar_mul(y[:], acc[:], gs_sb[:, t : t + 1])
            else:
                nc.scalar.activation(y[:], acc[:], ACT.Copy, scale=gs_sb[:, t : t + 1])
            ys.append(y)

        ds_picked = sb("ds_picked", [P, S], U8, tag="xs_picked")
        nc.vector.tensor_copy(ds_picked[:], ds_win[:].indirect(lists["k1"][:]))
        ds_dealt = sb("ds_dealt", [P, S], U8, tag="x_win")
        nc.vector.tensor_copy(
            ds_dealt[:].rearrange("p (t m) -> p t m", t=PACK), ds_picked[:].rearrange("p (m t) -> p t m", t=PACK)
        )
        place_rows(nc.sync, ds_dealt)

        d_picked = sb("d_picked", [P, S], U32)
        d_dealt = sb("d_dealt", [P, S], U32)
        nc.vector.tensor_copy(d_picked[:], d_win[:].indirect(lists["k1"][:]))
        nc.vector.tensor_copy(
            d_dealt[:].bitcast(I32).rearrange("p (t b i) -> p b t i", t=PACK, i=4),
            d_picked[:].bitcast(I32).rearrange("p (b i t) -> p b t i", t=PACK, i=4),
        )

        for half in range(2):
            for t in range(PACK):
                fetch_kind(t, half)
        twice_not_negative = sb("twice_not_negative", [P, PACK], F32, tag="ws_raw")
        nc.gpsimd.tensor_scalar(twice_not_negative[:], gs_sb[:], 0.0, 2.0, ALU.is_ge, ALU.mult)
        sign = sb("sign", [P, CW, PACK], BF16, tag="w_raw")
        nc.gpsimd.tensor_scalar(
            sign[:], twice_not_negative[:].unsqueeze(1).to_broadcast([P, CW, PACK]), 1.0, -1.0, ALU.mult, ALU.add
        )

        diff = []
        for half in range(2):
            other = sb("other%d" % half, [P, PACK, HALF], F32)
            diff.append(sb("diff%d" % half, [P, PACK, HALF], F32))
            for t in range(PACK):
                make_part(t, half)
            for t in range(PACK):
                nc.scalar.activation(other[:, t, :], ys[t][:].indirect(entries(lists["n2"], half * HALF, HALF)), ACT.Copy)
            for t in range(PACK):
                nc.vector.tensor_tensor(diff[half][:, t, :], part[half][:, t, :], other[:, t, :], ALU.add)

        h_acc = []
        for c in range(NCH):
            half, within = divmod(c * CW, HALF)
            size = sb("size%d" % c, [P, CW, PACK], BF16)
            nc.scalar.activation(four_at_a_time_out(size), four_at_a_time_in(diff[half][:, :, within : within + CW]), ACT.Abs)
            z = sb("z%d" % c, [P, CW, PACK], BF16)
            nc.vector.tensor_tensor(z[:], size[:], sign[:], ALU.mult)
            z_words = sb("z_words%d" % c, [P, CW], U32)
            z_scales = sb("z_scales%d" % c, [P, CW], U8)
            nc.vector.quantize_mx(
                out=z_words[:].bitcast(FP8X4), scales=z_scales[:], in_=z[:].rearrange("p c t -> p (c t)")
            )
            for pair in range(2):
                acc = bank((4 + 2 * c + pair) % 8, 2 * CW, "h_acc%d_%d" % (c, pair))
                for u in range(2):
                    cols = slice((2 * pair + u) * P, (2 * pair + u + 1) * P)
                    nc.tensor.matmul_mx(
                        out=acc[:, u * CW : (u + 1) * CW], lhsT=d_dealt[:, cols].bitcast(FP8X4), lhsT_scale=ds_dealt[:, cols],
                        rhs=z_words[:].bitcast(FP8X4), rhs_scale=z_scales[:], start=True, stop=True,
                    )
                h_acc.append(acc)

        h = sb("h", [P, PACK, S], F32)
        for c in range(NCH):
            for pair in range(2):
                dst = h[:, 2 * pair : 2 * pair + 2, c * CW : (c + 1) * CW]
                src = h_acc[2 * c + pair][:].rearrange("p (u c) -> p u c", u=2)
                if pair == 1 and c >= 2:
                    nc.vector.tensor_scalar_mul(dst, src, 0.0625)
                else:
                    nc.scalar.activation(dst, src, ACT.Copy, scale=0.0625)

        out_rows = out_0.rearrange("(p t) c -> p t c", t=PACK)
        out_words = out_1[0].rearrange("p n r -> p (n r)").bitcast(I32)
        o_words = sb("o_words", [P, S], U32)
        o_scales = sb("o_scales", [P, S], U8)
        for c in range(NCH):
            c0 = c * CW
            half, within = divmod(c0, HALF)
            if within == 0:
                near = sb("near%d" % half, [P, PACK, HALF], F32)
                far = sb("far%d" % half, [P, PACK, HALF], F32)
                for t in range(PACK):
                    picked = h[:, t, :].indirect(entries(lists["n3"], c0, HALF))
                    if t == PACK - 1 and half == 0:
                        nc.scalar.activation(near[:, t, :], picked, ACT.Copy)
                    else:
                        nc.vector.tensor_copy(near[:, t, :], picked)
                    nc.scalar.activation(far[:, t, :], h[:, t, :].indirect(entries(lists["n4"], c0, HALF)), ACT.Copy)
            gap = sb("gap%d" % c, [P, PACK, CW], F32)
            bent = sb("bent%d" % c, [P, PACK, CW], F32)
            res = sb("res%d" % c, [P, PACK, CW], F32)
            nc.vector.tensor_tensor(gap[:], near[:, :, within : within + CW], h[:, :, c0 : c0 + CW], ALU.subtract)
            nc.scalar.activation(bent[:], gap[:], ACT.Tanh)
            nc.vector.tensor_tensor(res[:], bent[:], far[:, :, within : within + CW], ALU.mult)
            nc.sync.dma_start(out_rows[:, :, c0 : c0 + CW], res[:])
            rounded = sb("rounded%d" % c, [P, CW, PACK], BF16)
            if c < NCH - 1:
                nc.scalar.activation(four_at_a_time_out(rounded), four_at_a_time_in(res[:]), ACT.Copy)
            else:
                nc.vector.tensor_copy(four_at_a_time_out(rounded), four_at_a_time_in(res[:]))
            nc.vector.quantize_mx(
                out=o_words[:, c0 : c0 + CW].bitcast(FP8X4), scales=o_scales[:, c0 : c0 + CW], in_=rounded[:].rearrange("p c t -> p (c t)")
            )
            if within > 0:
                cols = slice(half * HALF, (half + 1) * HALF)
                nc.sync.dma_start(out_words[:, cols], o_words[:, cols].bitcast(I32))
        for q in range(4):
            queue = nc.scalar if q % 2 == 0 else nc.sync
            queue.dma_start(out_2[0, 4 * q : 4 * q + 4, :].bitcast(I32), o_scales[32 * q : 32 * q + 4, :].bitcast(I32))
